import numpy as np
import ml_dtypes


def mxq(x, axis, fmt="e4m3"):
    dtype, down = {"e4m3": (ml_dtypes.float8_e4m3fn, 7), "e5m2": (ml_dtypes.float8_e5m2, 14)}[fmt]
    v = np.moveaxis(np.asarray(x, np.float32).astype(ml_dtypes.bfloat16).astype(np.float64), axis, -1)
    blocks = v.reshape(v.shape[:-1] + (-1, 32))
    amax = np.abs(blocks).max(-1, keepdims=True)
    byte = np.maximum(np.where(amax > 0, np.frexp(amax)[1] - 1 + 127, 0) - down, 1)
    scale = np.exp2(byte - 127.0)
    codes = (blocks / scale).astype(np.float32).astype(dtype).astype(np.float64)
    return np.moveaxis((codes * scale).reshape(v.shape), -1, axis)


WIDE = False


def mx_kscale(k, group=512):
    if not WIDE:
        return np.ones(k)
    levels = np.array([10, -10, 5, -5, 0])
    if group != 512:
        return np.exp2(np.random.permutation(np.resize(levels, k // group))).repeat(group)
    if k % 512:
        return np.exp2(np.random.permutation(np.resize(levels, k // 32))).repeat(32)
    a = np.empty((k // 512, 16))
    for p in range(k // 512):
        a[p, :8] = np.random.permutation(np.resize(levels, 8))
        for g in range(8):
            far = levels[np.abs(levels - a[p, g]) >= 10]
            a[p, g + 8] = far[np.random.randint(len(far))]
    return np.exp2(a.ravel()).repeat(32)


def f64(x):
    return np.asarray(x).astype(np.float64)


def striped(idx):
    return np.tile(np.asarray(idx).reshape(-1, 16).T, (8, 1)).astype(np.uint16)


def unstriped(offs):
    return offs[:16].T.reshape(-1).astype(np.int64)


H, KV, D, NQ, N = 8, 2, 128, 512, 512
CAP = 2.0


def setup_inputs():
    n = np.random.standard_normal
    s = mx_kscale(D, 0)[:, None]
    u = mx_kscale(N)
    t = np.random.uniform(0.5, 2.0, N) * u
    v = n((KV, N, 128))
    v[:, :, 127] = 1.0
    return {
        "qT": (n((H, D, NQ)) * s * (0.70 / np.sqrt(D))).astype(np.float32),
        "kT": (n((KV, D, N)) / s).astype(np.float32),
        "t": t.reshape(N, 1).astype(np.float32),
        "v": (v / t[:, None]).astype(np.float32),
        "kb": (0.5 * n((N, 1))).astype(np.float32),
        "mask": (np.arange(N)[:, None] <= np.sort(np.random.randint(N // 4, N, NQ))[None, :]).astype(np.float32),
    }


def reference(qT, kT, t, v, kb, mask):
    a = np.repeat(mxq(f64(kT), 1, "e4m3"), H // KV, 0).transpose(0, 2, 1) @ mxq(f64(qT), 1, "e4m3")
    a = a + f64(kb)
    a = CAP * np.tanh(a / CAP)
    p = np.square(np.maximum(a, 0.0))
    p = p * f64(mask)
    w = p * f64(t)
    y = mxq(w, 1, "e4m3").transpose(0, 2, 1) @ np.repeat(mxq(f64(v), 1, "e4m3"), H // KV, 0)
    y = y / (y[:, :, 127:128] + 1.0)
    return y

from contextlib import ExitStack

import concourse.mybir as mybir

F32 = mybir.dt.float32
BF16 = mybir.dt.bfloat16
U32 = mybir.dt.uint32
I32 = mybir.dt.int32
U8 = mybir.dt.uint8
FP8X4 = mybir.dt.float8_e4m3fn_x4
ALU = mybir.AluOpType
ACT = mybir.ActivationFunctionType

H, KV, D, NQ, N = 8, 2, 128, 512, 512
CAP = 2.0
P = 128
PACK = 4
ROWS = D // PACK
SET = P // ROWS
W = 128
FLOPS = 2 * 2 * H * NQ * N * D

CHUNKS = [1,1,1,1,1,1,1,2]
NSQ = [1,2,2,1,1,2,2,2]
ORDER = "cK0:D cK1:A qK:D cq01:D cq00:A qq00:D qq01:D M00:P rep:A S0:D S1:A T00:A M01:P M02:P cv:D T01:A S2:A T02:A S3:D M10:P P000:D qv:D cq1:D M03:P T10:A T03:A M11:P M20:P T11:A T20:A M12:P P010:D M21:P T12:A M30:P T21:A qq1:D M13:P M22:P T30:A M31:P T13:A T22:A T31:A Q00:D M40:P T40:A M23:P M32:P W10:D T23:A M41:P M50:P X00:D T32:A Q10:A T41:A Y00:P Q11:D T50:A M33:P D00:A T33:A W20:D M42:P M51:P T42:A T51:A M60:P R00:D X10:D W30:D M43:P Q20:A Y10:P D10:D M52:P Q21:D T60:A E00:D M61:P X20:D T43:A M70:P T52:A R10:D T61:A M53:P Q30:A M62:P W40:D X30:D Y20:P T70:A T53:A M71:P O00:S D20:D Y30:P E10:D T62:A T71:A M63:P O10:S R20:D W50:D Q40:A D30:D M72:P T63:A E20:D T72:A M73:P Q50:A X40:D Y40:P O20:S R30:D W60:D Q51:A E30:D T73:A X50:D P700:D D40:D P710:D P701:D Y50:P P711:D O30:S D50:D Q60:A Q61:A X60:D Q70:A Q71:A R40:D R50:D X70:D E40:D O40:S Y60:P D60:D Y70:P E50:A O50:S X71:D R60:D D70:D Y71:P R70:D D71:D E60:A E70:A O60:S R71:D E71:D O70:S O71:S"


def tile_rows_a_relu2_kb_mask_cap_kernel(tc, qT, kT, t, v, kb, mask, out):
    nc = tc.nc
    with ExitStack() as ctx:
        sb = ctx.enter_context(tc.tile_pool(name="sb", bufs=1))
        ps = ctx.enter_context(tc.psum_pool(name="ps", bufs=1))
        ctx.enter_context(tc.manual_schedule())

        def tiles(name, count, shape, dtype):
            return [sb.tile(shape, dtype, name="%s%d" % (name, i), align_bytes=64) for i in range(count)]

        t4, kb4, t_x4, t_abs, half, root, sgn01, sgn, kb_half, warm_in, warm_out = tiles("small", 11, [P, PACK], F32)
        k_raw = sb.tile([3 * ROWS, PACK, N], F32, align_bytes=64)
        k16 = sb.tile([3 * ROWS, PACK, W, PACK], BF16, align_bytes=64)
        kq = tiles("kq", 2, [P, N + N // 4], U32)
        q0_raw = tiles("q0_raw", 2, [P, PACK, NQ // 2], F32)
        q1_raw = sb.tile([P, PACK, NQ], F32, align_bytes=64)
        q16 = tiles("q16", 2, [P, NQ, PACK], BF16)
        q_codes = tiles("q_codes", 2, [P, NQ], U32)
        q_scales = tiles("q_scales", 2, [P, NQ], U8)
        m_raw = tiles("m_raw", 2, [P, 2, NQ], F32)
        s_mask = sb.tile([P, 2, 2, NQ], F32, align_bytes=64)
        v_raw = sb.tile([P, KV, PACK, D], F32, align_bytes=64)
        v16 = sb.tile([P, KV, D, PACK], BF16, align_bytes=64)
        v_codes = sb.tile([P, KV * D], U32, align_bytes=64)
        v_scales = sb.tile([P, KV * D], U8, align_bytes=64)
        th = tiles("th", H, [P, 2, 2, NQ], F32)
        u = tiles("u", 4, [P, 2, NQ, 2], F32)
        w16 = tiles("w16", 4, [P, NQ, PACK], BF16)
        w_codes = tiles("w_codes", H, [P, NQ], U32)
        w_scales = tiles("w_scales", H, [P, NQ], U8)
        den = tiles("den", H, [P, PACK], F32)
        rec = tiles("rec", H, [P, PACK], F32)
        res = tiles("res", H, [P, NQ // W, D], F32)
        bank = [ps.tile([P, NQ], F32, name="bank%d" % i) for i in range(5)]
        tile_banks = [[bank[0], bank[1]], [bank[2]], [bank[3]], [bank[4]]]
        y_banks = [ps.tile([P, NQ // W, D], F32, name="y%d" % i) for i in range(3)]

        k_view = kT.rearrange("g (p j) n -> g p j n", j=PACK)
        nc.scalar.dma_start(out=t4[:], in_=t.rearrange("(p j) o -> p (j o)", j=PACK))
        nc.sync.dma_start(out=k_raw[0:ROWS], in_=k_view[0])
        nc.scalar.dma_start(out=k_raw[2 * ROWS : 3 * ROWS], in_=k_view[1])
        nc.scalar.dma_start(out=kb4[:], in_=kb.rearrange("(p j) o -> p (j o)", j=PACK))
        q_sets = qT.rearrange("(s g) (p j) n -> s (g p) j n", g=SET, j=PACK)
        for c in range(2):
            nc.sync.dma_start(out=q0_raw[c][:], in_=q_sets[0][:, :, c * 256 : (c + 1) * 256])
        m_view = mask.rearrange("(p r) q -> p r q", r=PACK)
        nc.sync.dma_start(out=m_raw[0][:], in_=m_view[:, 0:2, :])
        nc.sync.dma_start(out=v_raw[:], in_=v.rearrange("g (p j) e -> p g j e", j=PACK))
        nc.sync.dma_start(out=m_raw[1][:], in_=m_view[:, 2:4, :])
        nc.sync.dma_start(out=q1_raw[:], in_=q_sets[1])

        nc.vector.memset(warm_in[:], 0.0)
        nc.scalar.activation(out=warm_out[:], in_=warm_in[:], func=ACT.Tanh)
        nc.gpsimd.memset(half[:], 0.5)
        nc.vector.memset(k_raw[ROWS : 2 * ROWS], 0.0)
        nc.vector.memset(kq[0][0 : 3 * ROWS, N:], 0)
        nc.vector.tensor_scalar(out=t_x4[:], in0=t4[:], scalar1=CAP * CAP, scalar2=None, op0=ALU.mult)
        nc.vector.tensor_scalar(out=sgn01[:], in0=t4[:], scalar1=0.0, scalar2=2.0, op0=ALU.is_ge, op1=ALU.mult)
        nc.vector.scalar_tensor_tensor(out=t_abs[:], in0=t_x4[:], scalar=-1.0, in1=t_x4[:], op0=ALU.mult, op1=ALU.max)
        nc.gpsimd.tensor_tensor(out=root[:], in0=t_abs[:], in1=half[:], op=ALU.pow)
        nc.vector.tensor_scalar(out=kb_half[:], in0=kb4[:], scalar1=1.0 / CAP, scalar2=None, op0=ALU.mult)
        nc.vector.tensor_scalar(out=sgn[:], in0=sgn01[:], scalar1=-1.0, scalar2=None, op0=ALU.add)

        def cast(eng, dst, src):
            if eng == "A":
                nc.scalar.copy(out=dst, in_=src)
            else:
                nc.vector.tensor_copy(out=dst, in_=src)

        def quant(codes, scales, src):
            nc.vector.quantize_mx(out=codes.bitcast(FP8X4), scales=scales, in_=src)

        def keys(h):
            g = h % SET
            home = kq[0] if (h // SET == 0) != (g == 2) else kq[1]
            return home[g * ROWS : (g + 1) * ROWS]

        def spread(queue, kv):
            for h in range(kv * SET, (kv + 1) * SET):
                if h % SET != 2 * kv:
                    queue.dma_start(out=keys(h).bitcast(I32), in_=kq[0][2 * kv * ROWS : (2 * kv + 1) * ROWS].bitcast(I32))

        ybank = {}
        for item in ORDER.split():
            name, eng = item.split(":")
            kind = name[0]
            if name[:2] == "cK":
                s0, s1 = (0, 80) if name[2] == "0" else (80, W)
                cast(eng, k16[:, :, s0:s1, :].rearrange("p r s j -> p s r j"),
                     k_raw[:, :, PACK * s0 : PACK * s1].rearrange("p j (s r) -> p s r j", r=PACK))
            elif name == "qK":
                quant(kq[0][0 : 3 * ROWS, 0:N], kq[0][0 : 3 * ROWS, N:].bitcast(U8), k16[:].rearrange("p r s j -> p (r s j)"))
            elif name[:2] == "qK":
                r = int(name[2])
                cols = slice(r * W, (r + 1) * W)
                quant(kq[0][0 : 3 * ROWS, cols], kq[0][0 : 3 * ROWS, N:].bitcast(U8)[:, cols],
                      k16[:, r].rearrange("p s j -> p (s j)"))
            elif name == "rep":
                spread(nc.scalar, 0)
                spread(nc.sync, 1)
            elif name[:3] == "cq0":
                i = int(name[3])
                cast(eng, q16[0][:, 256 * i : 256 * (i + 1), :], q0_raw[i][:].rearrange("p j n -> p n j"))
            elif name[:3] == "qq0":
                cols = slice(256 * int(name[3]), 256 * (int(name[3]) + 1))
                quant(q_codes[0][:, cols], q_scales[0][:, cols], q16[0][:, cols, :].rearrange("p n j -> p (n j)"))
            elif name == "cq1":
                cast(eng, q16[1][:], q1_raw[:].rearrange("p j n -> p n j"))
            elif name == "qq1":
                quant(q_codes[1][:], q_scales[1][:], q16[1][:].rearrange("p n j -> p (n j)"))
            elif name == "cv":
                nc.vector.tensor_tensor(out=v16[:], in0=v_raw[:].rearrange("p g j e -> p g e j"),
                                        in1=sgn[:].unsqueeze(1).unsqueeze(1).to_broadcast([P, KV, D, PACK]), op=ALU.mult)
            elif name == "qv":
                quant(v_codes[:], v_scales[:], v16[:].rearrange("p g e j -> p (g e j)"))
            elif kind == "S":
                r = int(name[1])
                if eng == "A":
                    nc.scalar.activation(out=s_mask[:, r % 2, r // 2, :], in_=m_raw[r // 2][:, r % 2, :], func=ACT.Copy, scale=root[:, r : r + 1])
                else:
                    nc.vector.tensor_scalar(out=s_mask[:, r % 2, r // 2, :], in0=m_raw[r // 2][:, r % 2, :],
                                            scalar1=root[:, r : r + 1], scalar2=None, op0=ALU.mult)
            elif kind == "M" or kind == "T":
                h, r = int(name[1]), int(name[2])
                g = h % SET
                scores = tile_banks[g][r % len(tile_banks[g])]
                q0, q1 = (0, NQ) if len(name) == 3 else (256 * int(name[3]), 256 * (int(name[3]) + 1))
                if kind == "T":
                    nc.scalar.activation(out=th[h][:, r % 2, r // 2, q0:q1], in_=scores[:, q0:q1], func=ACT.Tanh,
                                         bias=kb_half[:, r : r + 1], scale=1.0 / CAP)
                else:
                    rows = slice(g * ROWS, (g + 1) * ROWS)
                    kcols = slice(r * W, (r + 1) * W)
                    for c in range(q0, q1, W):
                        nc.tensor.matmul_mx(out=scores[:, c : c + W], lhsT=keys(h)[:, kcols].bitcast(FP8X4),
                                            lhsT_scale=keys(h)[:, N:].bitcast(U8)[:, kcols],
                                            rhs=q_codes[h // SET][rows, c : c + W].bitcast(FP8X4),
                                            rhs_scale=q_scales[h // SET][rows, c : c + W], start=True, stop=True)
            elif kind == "P":
                h, a, c = int(name[1]), int(name[2]), int(name[3])
                wd = NQ // CHUNKS[h]
                cols = slice(c * wd, (c + 1) * wd)
                nc.vector.scalar_tensor_tensor(out=u[h % 4][:, a, cols, :],
                                               in0=th[h][:, :, a, cols].rearrange("p e q -> p q e"),
                                               scalar=0.0, in1=s_mask[:, :, a, cols].rearrange("p e q -> p q e"),
                                               op0=ALU.max, op1=ALU.mult)
            elif kind == "W":
                h = int(name[1])
                nc.vector.scalar_tensor_tensor(out=u[h % 4][:].rearrange("p a q e -> p (a q) e"),
                                               in0=th[h][:].rearrange("p e a q -> p (a q) e"),
                                               scalar=0.0, in1=s_mask[:].rearrange("p e a q -> p (a q) e"),
                                               op0=ALU.max, op1=ALU.mult)
            elif kind == "Q":
                h, s = int(name[1]), int(name[2])
                wd = NQ // NSQ[h]
                cols = slice(s * wd, (s + 1) * wd)
                src = u[h % 4][:, :, cols, :].rearrange("p a q e -> p q a e")
                dst = w16[h % 4][:, cols, :].rearrange("p q (a e) -> p q a e", e=2)
                if eng == "A":
                    nc.scalar.activation(out=dst, in_=src, func=ACT.Square)
                else:
                    nc.vector.tensor_tensor(out=dst, in0=src, in1=src, op=ALU.mult)
            else:
                h, c = int(name[1]), int(name[2])
                wd = NQ // CHUNKS[h]
                cols = slice(c * wd, (c + 1) * wd)
                blocks = slice(c * wd // W, (c + 1) * wd // W)
                nb = wd // W
                if kind == "X":
                    quant(w_codes[h][:, cols], w_scales[h][:, cols], w16[h % 4][:, cols, :].rearrange("p q j -> p (q j)"))
                elif kind == "Y":
                    ybank[(h, c)] = y_banks[(sum(CHUNKS[:h]) + c) % 3]
                    vcols = slice((h // SET) * D, (h // SET + 1) * D)
                    for b in range(blocks.start, blocks.stop):
                        nc.tensor.matmul_mx(out=ybank[(h, c)][:, b, :], lhsT=w_codes[h][:, b * W : (b + 1) * W].bitcast(FP8X4),
                                            lhsT_scale=w_scales[h][:, b * W : (b + 1) * W],
                                            rhs=v_codes[:, vcols].bitcast(FP8X4), rhs_scale=v_scales[:, vcols],
                                            start=True, stop=True)
                elif kind == "D" and eng == "A":
                    nc.scalar.activation(out=den[h][:, blocks], in_=ybank[(h, c)][:, blocks, D - 1], func=ACT.Identity, bias=1.0)
                elif kind == "D":
                    nc.vector.tensor_scalar(out=den[h][:, blocks], in0=ybank[(h, c)][:, blocks, D - 1], scalar1=1.0, scalar2=None, op0=ALU.add)
                elif kind == "R":
                    nc.vector.reciprocal(out=rec[h][:, blocks], in_=den[h][:, blocks])
                elif kind == "E":
                    if eng == "A":
                        for b in range(blocks.start, blocks.stop):
                            nc.scalar.activation(out=res[h][:, b, :], in_=ybank[(h, c)][:, b, :], func=ACT.Copy, scale=rec[h][:, b : b + 1])
                    else:
                        nc.vector.tensor_tensor(out=res[h][:, blocks, :], in0=ybank[(h, c)][:, blocks, :],
                                                in1=rec[h][:, blocks].unsqueeze(2).to_broadcast([P, nb, D]), op=ALU.mult)
                else:
                    nc.sync.dma_start(out=out[h, cols, :].rearrange("(c p) e -> p c e", p=W), in_=res[h][:, blocks, :])
